import numpy as np
import ml_dtypes


def mxq(x, axis, fmt="e4m3"):
    dtype, down = {"e4m3": (ml_dtypes.float8_e4m3fn, 7), "e5m2": (ml_dtypes.float8_e5m2, 14)}[fmt]
    v = np.moveaxis(np.asarray(x, np.float32).astype(ml_dtypes.bfloat16).astype(np.float64), axis, -1)
    blocks = v.reshape(v.shape[:-1] + (-1, 32))
    amax = np.abs(blocks).max(-1, keepdims=True)
    byte = np.maximum(np.where(amax > 0, np.frexp(amax)[1] - 1 + 127, 0) - down, 1)
    scale = np.exp2(byte - 127.0)
    codes = (blocks / scale).astype(np.float32).astype(dtype).astype(np.float64)
    return np.moveaxis((codes * scale).reshape(v.shape), -1, axis)


WIDE = False


def mx_kscale(k):
    if not WIDE:
        return np.ones(k)
    levels = np.array([10, -10, 5, -5, 0])
    if k % 512:
        return np.exp2(np.random.permutation(np.resize(levels, k // 32))).repeat(32)
    a = np.empty((k // 512, 16))
    for p in range(k // 512):
        a[p, :8] = np.random.permutation(np.resize(levels, 8))
        for g in range(8):
            far = levels[np.abs(levels - a[p, g]) >= 10]
            a[p, g + 8] = far[np.random.randint(len(far))]
    return np.exp2(a.ravel()).repeat(32)


def f64(x):
    return np.asarray(x).astype(np.float64)


def striped(idx):
    return np.tile(np.asarray(idx).reshape(-1, 16).T, (8, 1)).astype(np.uint16)


def unstriped(offs):
    return offs[:16].T.reshape(-1).astype(np.int64)


E2M1 = np.array([0.0, 0.5, 1.0, 1.5, 2.0, 3.0, 4.0, 6.0, -0.0, -0.5, -1.0, -1.5, -2.0, -3.0, -4.0, -6.0])


def pack_weight(w, fmt):
    k, n = w.shape
    w = f64(np.asarray(w, np.float32).astype(ml_dtypes.bfloat16)).reshape(k // 32, 32, n)
    amax = np.abs(w).max(1)
    if fmt == "e4m3":
        byte = np.frexp(amax)[1] - 1 + 127 - 7
    else:
        mant, ex = np.frexp(amax / 6.0)
        byte = np.where(mant > 0.5, ex, ex - 1) + 127
    byte = np.clip(np.where(amax > 0, byte, 1), 1, 254)
    scaled = (w * np.exp2(127.0 - byte)[:, None, :]).reshape(k, n).astype(np.float32)
    by_word = np.ascontiguousarray(scaled.reshape(k // 512, 128, 4, n).transpose(0, 1, 3, 2))
    if fmt == "e4m3":
        words = by_word.astype(ml_dtypes.float8_e4m3fn).view(np.uint8)
    else:
        c = by_word.astype(ml_dtypes.float4_e2m1fn).view(np.uint8) & 0xF
        words = (c[..., 0::2] | (c[..., 1::2] << 4)).reshape(k // 512, 128, 2 * n)
    return np.ascontiguousarray(words), np.ascontiguousarray(byte.astype(np.uint8).reshape(k // 512, 16, n))


def unpack_weight(words, scales, fmt):
    g, _, n = scales.shape
    words = np.ascontiguousarray(words).reshape(g, 128, n, -1)
    if fmt == "e4m3":
        vals = words.view(ml_dtypes.float8_e4m3fn).astype(np.float64)
    else:
        nib = np.empty((g, 128, n, 4), np.uint8)
        nib[..., 0::2] = words & 0xF
        nib[..., 1::2] = words >> 4
        vals = E2M1[nib]
    vals = vals * np.repeat(np.exp2(scales.astype(np.float64) - 127.0), 8, axis=1)[..., None]
    return vals.transpose(0, 1, 3, 2).reshape(g * 512, n)


def silu(v):
    return v / (1.0 + np.exp(-v))


K, T, J, B, N = 1024, 1024, 512, 64, 512


def setup_inputs():
    n = np.random.standard_normal
    idx = (np.random.permutation(T // 8)[:J // 8, None] * 8 + np.arange(8)).reshape(-1)
    fk = mx_kscale(K)
    xtp = pack_weight(n((K, T)) / fk[:, None], "e4m3")
    return {
        "xt_words": xtp[0],
        "xt_scales": xtp[1],
        "wa": (n((K, N)) * 1 / np.sqrt(K) * fk[:, None]).astype(np.float32),
        "bw": (np.random.uniform(0.4, 1.4, (N, B))).astype(np.float32),
        "res": (1.0 * n((N, T))).astype(np.float32),
        "offs": striped(idx),
    }


def reference(xt_words, xt_scales, wa, bw, res, offs):
    idx = unstriped(offs)
    xtu = unpack_weight(xt_words, xt_scales, "e4m3")
    waq = mxq(f64(wa), 0, "e4m3")
    xtidxg = xtu[:, idx]
    p = waq.T @ xtidxg
    br = np.repeat(f64(bw), J // B, axis=1)
    d = silu(p * br)
    dp = np.zeros((N, T))
    dp[:, idx] = d
    y = 0.3 * f64(res) + dp
    return y

@@ -1,0 +1,156 @@
+from contextlib import ExitStack
+
+import concourse.mybir as mybir
+
+K, T, J, B, N = 1024, 1024, 512, 64, 512
+FLOPS = 2 * K * N * J
+
+F32 = mybir.dt.float32
+BF16 = mybir.dt.bfloat16
+I32 = mybir.dt.int32
+U32 = mybir.dt.uint32
+U16 = mybir.dt.uint16
+U8 = mybir.dt.uint8
+FP8X4 = mybir.dt.float8_e4m3fn_x4
+MULT = mybir.AluOpType.mult
+ADD = mybir.AluOpType.add
+SILU = mybir.ActivationFunctionType.Silu
+
+P = 128
+PACK = 4
+PASSES = K // (P * PACK)
+TILES = N // P
+RUN = J // B
+RES_SCALE = 0.3
+
+
+def tile_moe_block_routed_expert_kernel(tc, xt_words, xt_scales, wa, bw, res, offs, out):
+    nc = tc.nc
+    with ExitStack() as ctx:
+        held = ctx.enter_context(tc.tile_pool(name="held", bufs=1))
+        psum = ctx.enter_context(tc.psum_pool(name="psum", bufs=1))
+
+        offsets = held.tile([P, J // 16], U16, name="offsets")
+        x_planes = held.tile([P, T], U8, name="x_planes", align_bytes=64)
+        x_words = [held.tile([P, T], U32, name="x_words%d" % a, align_bytes=64) for a in range(PASSES)]
+        g_planes = held.tile([P, J], U8, name="g_planes", align_bytes=64)
+        g_words = [held.tile([P, J], U32, name="g_words%d" % a, align_bytes=64) for a in range(PASSES)]
+        windows = [held.tile([P, T], F32, name="window%d" % i, align_bytes=64) for i in range(2)]
+        bw_sb = held.tile([P, TILES, B], F32, name="bw_sb")
+        res_sb = [held.tile([P, T], F32, name="res_sb%d" % i, align_bytes=64) for i in range(TILES)]
+        warm = held.tile([P, 1], F32, name="warm")
+        warm_out = held.tile([P, 1], F32, name="warm_out")
+
+        nc.vector.memset(x_planes[:].bitcast(I32), 0)
+        nc.vector.memset(warm[:], 0.0)
+        nc.scalar.activation(out=warm_out[:], in_=warm[:], func=SILU)
+        for w in windows:
+            nc.vector.memset(w[:], 0.0)
+
+        def load_words(a):
+            nc.sync.dma_start(
+                out=x_words[a][:].bitcast(I32),
+                in_=xt_words[a].rearrange("p c r -> p (c r)").bitcast(I32),
+            )
+
+        wa_rows = wa.rearrange("(a p j) n -> a p j n", a=PASSES, j=PACK)
+        raw = {}
+
+        def load_wa(first, count):
+            for a in range(PASSES):
+                piece = held.tile([P, PACK, count * P], F32, name="raw%d_%d" % (first, a), align_bytes=64)
+                nc.sync.dma_start(out=piece[:], in_=wa_rows[a, :, :, first * P : (first + count) * P])
+                for i in range(count):
+                    raw[(first + i, a)] = piece[:, :, i * P : (i + 1) * P]
+
+        def load_res(i):
+            nc.sync.dma_start(out=res_sb[i][:], in_=res[i * P : (i + 1) * P, :])
+
+        nc.sync.dma_start(offsets[:], offs)
+        load_words(0)
+        for q in range(4):
+            nc.sync.dma_start(
+                out=x_planes[32 * q : 32 * q + 4 * PASSES, :].bitcast(I32),
+                in_=xt_scales[:, 4 * q : 4 * q + 4, :].bitcast(I32),
+            )
+        load_words(1)
+        load_wa(0, 1)
+        nc.sync.dma_start(out=bw_sb[:], in_=bw.rearrange("(i p) b -> p i b", p=P))
+        load_wa(1, 1)
+        load_res(0)
+        load_wa(2, 2)
+        for i in range(1, TILES):
+            load_res(i)
+
+        nc.vector.tensor_copy(g_planes[:], x_planes[:].indirect(offsets[:]))
+        for a in range(PASSES):
+            nc.vector.tensor_copy(g_words[a][:], x_words[a][:].indirect(offsets[:]))
+
+        acc = {}
+        gated = {}
+        act = {}
+
+        def product(i):
+            acc[i] = psum.tile([P, J], F32, name="acc%d" % i)
+            for a in range(PASSES):
+                grouped = held.tile([P, P, PACK], BF16, name="grouped%d_%d" % (i, a), align_bytes=64)
+                nc.scalar.copy(
+                    out=grouped[:].rearrange("p (c u) j -> p c j u", u=4),
+                    in_=raw[(i, a)].rearrange("p j (c u) -> p c j u", u=4),
+                )
+                codes = held.tile([P, P], U32, name="codes%d_%d" % (i, a), align_bytes=64)
+                plane = held.tile([P, P], U8, name="plane%d_%d" % (i, a), align_bytes=64)
+                nc.vector.quantize_mx(
+                    out=codes[:].bitcast(FP8X4),
+                    scales=plane[:],
+                    in_=grouped[:].rearrange("p c j -> p (c j)"),
+                )
+                nc.tensor.matmul_mx(
+                    out=acc[i][:],
+                    lhsT=codes[:].bitcast(FP8X4),
+                    lhsT_scale=plane[:],
+                    rhs=g_words[a][:].bitcast(FP8X4),
+                    rhs_scale=g_planes[4 * a : P, :],
+                    start=(a == 0),
+                    stop=(a == PASSES - 1),
+                )
+
+        def activate(i):
+            gated[i] = held.tile([P, B, RUN], F32, name="gated%d" % i, align_bytes=64)
+            nc.vector.tensor_tensor(
+                out=gated[i][:],
+                in0=acc[i][:].rearrange("p (b e) -> p b e", e=RUN),
+                in1=bw_sb[:, i, :].unsqueeze(2).to_broadcast([P, B, RUN]),
+                op=MULT,
+            )
+            act[i] = held.tile([P, J], F32, name="act%d" % i, align_bytes=64)
+            nc.scalar.activation(out=act[i][:], in_=gated[i][:].rearrange("p b e -> p (b e)"), func=SILU)
+
+        def scatter(i):
+            nc.vector.tensor_copy(windows[i % 2][:].indirect(offsets[:]), act[i][:])
+
+        def finish(i, pieces):
+            width = T // pieces
+            for h in range(pieces):
+                cols = slice(h * width, (h + 1) * width)
+                total = held.tile([P, width], F32, name="total%d_%d" % (i, h), align_bytes=64)
+                nc.vector.scalar_tensor_tensor(
+                    out=total[:],
+                    in0=res_sb[i][:, cols],
+                    scalar=RES_SCALE,
+                    in1=windows[i % 2][:, cols],
+                    op0=MULT,
+                    op1=ADD,
+                )
+                nc.sync.dma_start(out=out[i * P : (i + 1) * P, cols], in_=total[:])
+
+        product(0)
+        activate(0)
+        product(1)
+        activate(1)
+        for i in range(TILES):
+            scatter(i)
+            if i + 2 < TILES:
+                product(i + 2)
+                activate(i + 2)
+            finish(i, 2 if i == TILES - 1 else 1)

@@ -14,6 +14,7 @@ U8 = mybir.dt.uint8
 FP8X4 = mybir.dt.float8_e4m3fn_x4
 MULT = mybir.AluOpType.mult
 ADD = mybir.AluOpType.add
+COPY = mybir.ActivationFunctionType.Copy
 SILU = mybir.ActivationFunctionType.Silu
 
 P = 128
@@ -35,15 +36,11 @@ def tile_moe_block_routed_expert_kernel(tc, xt_words, xt_scales, wa, bw, res, of
         x_words = [held.tile([P, T], U32, name="x_words%d" % a, align_bytes=64) for a in range(PASSES)]
         g_planes = held.tile([P, J], U8, name="g_planes", align_bytes=64)
         g_words = [held.tile([P, J], U32, name="g_words%d" % a, align_bytes=64) for a in range(PASSES)]
-        windows = [held.tile([P, T], F32, name="window%d" % i, align_bytes=64) for i in range(2)]
+        windows = [held.tile([P, T], F32, name="window%d" % i, align_bytes=64) for i in range(3)]
         bw_sb = held.tile([P, TILES, B], F32, name="bw_sb")
         res_sb = [held.tile([P, T], F32, name="res_sb%d" % i, align_bytes=64) for i in range(TILES)]
-        warm = held.tile([P, 1], F32, name="warm")
-        warm_out = held.tile([P, 1], F32, name="warm_out")
 
         nc.vector.memset(x_planes[:].bitcast(I32), 0)
-        nc.vector.memset(warm[:], 0.0)
-        nc.scalar.activation(out=warm_out[:], in_=warm[:], func=SILU)
         for w in windows:
             nc.vector.memset(w[:], 0.0)
 
@@ -56,12 +53,11 @@ def tile_moe_block_routed_expert_kernel(tc, xt_words, xt_scales, wa, bw, res, of
         wa_rows = wa.rearrange("(a p j) n -> a p j n", a=PASSES, j=PACK)
         raw = {}
 
-        def load_wa(first, count):
-            for a in range(PASSES):
-                piece = held.tile([P, PACK, count * P], F32, name="raw%d_%d" % (first, a), align_bytes=64)
-                nc.sync.dma_start(out=piece[:], in_=wa_rows[a, :, :, first * P : (first + count) * P])
-                for i in range(count):
-                    raw[(first + i, a)] = piece[:, :, i * P : (i + 1) * P]
+        def load_wa(first, count, a):
+            piece = held.tile([P, PACK, count * P], F32, name="raw%d_%d" % (first, a), align_bytes=64)
+            nc.sync.dma_start(out=piece[:], in_=wa_rows[a, :, :, first * P : (first + count) * P])
+            for i in range(count):
+                raw[(first + i, a)] = piece[:, :, i * P : (i + 1) * P]
 
         def load_res(i):
             nc.sync.dma_start(out=res_sb[i][:], in_=res[i * P : (i + 1) * P, :])
@@ -74,60 +70,80 @@ def tile_moe_block_routed_expert_kernel(tc, xt_words, xt_scales, wa, bw, res, of
                 in_=xt_scales[:, 4 * q : 4 * q + 4, :].bitcast(I32),
             )
         load_words(1)
-        load_wa(0, 1)
+        for a in range(PASSES):
+            load_wa(0, 1, a)
         nc.sync.dma_start(out=bw_sb[:], in_=bw.rearrange("(i p) b -> p i b", p=P))
-        load_wa(1, 1)
-        load_res(0)
-        load_wa(2, 2)
-        for i in range(1, TILES):
+        for a in range(PASSES):
+            load_wa(1, 1, a)
+        for a in range(PASSES):
+            load_wa(2, 2, a)
+        for i in range(TILES):
             load_res(i)
 
         nc.vector.tensor_copy(g_planes[:], x_planes[:].indirect(offsets[:]))
         for a in range(PASSES):
             nc.vector.tensor_copy(g_words[a][:], x_words[a][:].indirect(offsets[:]))
 
+        def cuts(i):
+            pieces = 1
+            return [(h * J // pieces, (h + 1) * J // pieces) for h in range(pieces)]
+
+        weights = {}
         acc = {}
-        gated = {}
         act = {}
 
-        def product(i):
-            acc[i] = psum.tile([P, J], F32, name="acc%d" % i)
+        def quantise(i):
+            grouped = held.tile([P, PASSES, P, PACK], BF16, name="grouped%d" % i, tag="grouped%d" % i, align_bytes=64)
+            codes = held.tile([P, PASSES * P], U32, name="codes%d" % i, align_bytes=64)
+            planes = held.tile([P, PASSES * P], U8, name="planes%d" % i, align_bytes=64)
+            together = 1 if i == 0 else PASSES
             for a in range(PASSES):
-                grouped = held.tile([P, P, PACK], BF16, name="grouped%d_%d" % (i, a), align_bytes=64)
-                nc.scalar.copy(
-                    out=grouped[:].rearrange("p (c u) j -> p c j u", u=4),
+                nc.scalar.activation(
+                    out=grouped[:, a, :, :].rearrange("p (c u) j -> p c j u", u=4),
                     in_=raw[(i, a)].rearrange("p j (c u) -> p c j u", u=4),
+                    func=COPY,
                 )
-                codes = held.tile([P, P], U32, name="codes%d_%d" % (i, a), align_bytes=64)
-                plane = held.tile([P, P], U8, name="plane%d_%d" % (i, a), align_bytes=64)
-                nc.vector.quantize_mx(
-                    out=codes[:].bitcast(FP8X4),
-                    scales=plane[:],
-                    in_=grouped[:].rearrange("p c j -> p (c j)"),
-                )
-                nc.tensor.matmul_mx(
-                    out=acc[i][:],
-                    lhsT=codes[:].bitcast(FP8X4),
-                    lhsT_scale=plane[:],
-                    rhs=g_words[a][:].bitcast(FP8X4),
-                    rhs_scale=g_planes[4 * a : P, :],
-                    start=(a == 0),
-                    stop=(a == PASSES - 1),
-                )
+                weights[(i, a)] = (codes[:, a * P : (a + 1) * P], planes[:, a * P : (a + 1) * P])
+                if (a + 1) % together == 0:
+                    first = a + 1 - together
+                    nc.vector.quantize_mx(
+                        out=codes[:, first * P : (a + 1) * P].bitcast(FP8X4),
+                        scales=planes[:, first * P : (a + 1) * P],
+                        in_=grouped[:, first : a + 1, :, :].rearrange("p a c j -> p (a c j)"),
+                    )
+
+        def product(i):
+            for lo, hi in cuts(i):
+                acc[(i, lo)] = psum.tile([P, hi - lo], F32, name="acc%d_%d" % (i, lo))
+            for a in range(PASSES):
+                codes, plane = weights[(i, a)]
+                for lo, hi in cuts(i):
+                    nc.tensor.matmul_mx(
+                        out=acc[(i, lo)][:],
+                        lhsT=codes.bitcast(FP8X4),
+                        lhsT_scale=plane,
+                        rhs=g_words[a][:, lo:hi].bitcast(FP8X4),
+                        rhs_scale=g_planes[4 * a : P, lo:hi],
+                        start=(a == 0),
+                        stop=(a == PASSES - 1),
+                    )
 
         def activate(i):
-            gated[i] = held.tile([P, B, RUN], F32, name="gated%d" % i, align_bytes=64)
-            nc.vector.tensor_tensor(
-                out=gated[i][:],
-                in0=acc[i][:].rearrange("p (b e) -> p b e", e=RUN),
-                in1=bw_sb[:, i, :].unsqueeze(2).to_broadcast([P, B, RUN]),
-                op=MULT,
-            )
+            gated = held.tile([P, J], F32, name="gated%d" % i, align_bytes=64)
             act[i] = held.tile([P, J], F32, name="act%d" % i, align_bytes=64)
-            nc.scalar.activation(out=act[i][:], in_=gated[i][:].rearrange("p b e -> p (b e)"), func=SILU)
+            for lo, hi in cuts(i):
+                blocks = (hi - lo) // RUN
+                nc.vector.tensor_tensor(
+                    out=gated[:, lo:hi].rearrange("p (b e) -> p b e", e=RUN),
+                    in0=acc[(i, lo)][:].rearrange("p (b e) -> p b e", e=RUN),
+                    in1=bw_sb[:, i, lo // RUN : hi // RUN].unsqueeze(2).to_broadcast([P, blocks, RUN]),
+                    op=MULT,
+                )
+                nc.scalar.activation(out=act[i][:, lo:hi], in_=gated[:, lo:hi], func=SILU)
 
         def scatter(i):
-            nc.vector.tensor_copy(windows[i % 2][:].indirect(offsets[:]), act[i][:])
+            for lo, hi in cuts(i):
+                nc.vector.tensor_copy(windows[i % 3][:].indirect(offsets[:, lo // 16 : hi // 16]), act[i][:, lo:hi])
 
         def finish(i, pieces):
             width = T // pieces
@@ -138,19 +154,35 @@ def tile_moe_block_routed_expert_kernel(tc, xt_words, xt_scales, wa, bw, res, of
                     out=total[:],
                     in0=res_sb[i][:, cols],
                     scalar=RES_SCALE,
-                    in1=windows[i % 2][:, cols],
+                    in1=windows[i % 3][:, cols],
                     op0=MULT,
                     op1=ADD,
                 )
                 nc.sync.dma_start(out=out[i * P : (i + 1) * P, cols], in_=total[:])
 
+        def finish_on_gpsimd(i):
+            nc.scalar.activation(out=res_sb[i][:], in_=res_sb[i][:], func=COPY, scale=RES_SCALE)
+            tag = "grouped%d" % (TILES - 1) if i == 0 else "total%d" % i
+            total = held.tile([P, T], F32, name="total%d" % i, tag=tag, align_bytes=64)
+            nc.gpsimd.tensor_tensor(out=total[:], in0=res_sb[i][:], in1=windows[i % 3][:], op=ADD)
+            nc.sync.dma_start(out=out[i * P : (i + 1) * P, :], in_=total[:])
+
+        quantise(0)
         product(0)
         activate(0)
+        quantise(1)
         product(1)
+        scatter(0)
         activate(1)
-        for i in range(TILES):
-            scatter(i)
-            if i + 2 < TILES:
-                product(i + 2)
-                activate(i + 2)
-            finish(i, 2 if i == TILES - 1 else 1)
+        for i in (2, 3):
+            quantise(i)
+            product(i)
+        scatter(1)
+        for i in (2, 3):
+            activate(i)
+        for i in (0, 1):
+            finish_on_gpsimd(i)
+        scatter(2)
+        scatter(3)
+        finish(2, 1)
+        finish(3, 2)

@@ -14,7 +14,6 @@ U8 = mybir.dt.uint8
 FP8X4 = mybir.dt.float8_e4m3fn_x4
 MULT = mybir.AluOpType.mult
 ADD = mybir.AluOpType.add
-COPY = mybir.ActivationFunctionType.Copy
 SILU = mybir.ActivationFunctionType.Silu
 
 P = 128
@@ -36,11 +35,15 @@ def tile_moe_block_routed_expert_kernel(tc, xt_words, xt_scales, wa, bw, res, of
         x_words = [held.tile([P, T], U32, name="x_words%d" % a, align_bytes=64) for a in range(PASSES)]
         g_planes = held.tile([P, J], U8, name="g_planes", align_bytes=64)
         g_words = [held.tile([P, J], U32, name="g_words%d" % a, align_bytes=64) for a in range(PASSES)]
-        windows = [held.tile([P, T], F32, name="window%d" % i, align_bytes=64) for i in range(3)]
+        windows = [held.tile([P, T], F32, name="window%d" % i, align_bytes=64) for i in range(2)]
         bw_sb = held.tile([P, TILES, B], F32, name="bw_sb")
         res_sb = [held.tile([P, T], F32, name="res_sb%d" % i, align_bytes=64) for i in range(TILES)]
 
+        warm = held.tile([P, 1], F32, name="warm")
+        warm_out = held.tile([P, 1], F32, name="warm_out")
         nc.vector.memset(x_planes[:].bitcast(I32), 0)
+        nc.vector.memset(warm[:], 0.0)
+        nc.scalar.activation(out=warm_out[:], in_=warm[:], func=SILU)
         for w in windows:
             nc.vector.memset(w[:], 0.0)
 
@@ -69,14 +72,13 @@ def tile_moe_block_routed_expert_kernel(tc, xt_words, xt_scales, wa, bw, res, of
                 out=x_planes[32 * q : 32 * q + 4 * PASSES, :].bitcast(I32),
                 in_=xt_scales[:, 4 * q : 4 * q + 4, :].bitcast(I32),
             )
+        nc.sync.dma_start(out=bw_sb[:], in_=bw.rearrange("(i p) b -> p i b", p=P))
         load_words(1)
         for a in range(PASSES):
             load_wa(0, 1, a)
-        nc.sync.dma_start(out=bw_sb[:], in_=bw.rearrange("(i p) b -> p i b", p=P))
-        for a in range(PASSES):
-            load_wa(1, 1, a)
-        for a in range(PASSES):
-            load_wa(2, 2, a)
+        for i in range(1, TILES):
+            for a in range(PASSES):
+                load_wa(i, 1, a)
         for i in range(TILES):
             load_res(i)
 
@@ -84,24 +86,19 @@ def tile_moe_block_routed_expert_kernel(tc, xt_words, xt_scales, wa, bw, res, of
         for a in range(PASSES):
             nc.vector.tensor_copy(g_words[a][:], x_words[a][:].indirect(offsets[:]))
 
-        def cuts(i):
-            pieces = 1
-            return [(h * J // pieces, (h + 1) * J // pieces) for h in range(pieces)]
-
         weights = {}
         acc = {}
-        act = {}
 
         def quantise(i):
-            grouped = held.tile([P, PASSES, P, PACK], BF16, name="grouped%d" % i, tag="grouped%d" % i, align_bytes=64)
+            grouped = held.tile([P, PASSES, P, PACK], BF16, name="grouped%d" % i, align_bytes=64)
             codes = held.tile([P, PASSES * P], U32, name="codes%d" % i, align_bytes=64)
             planes = held.tile([P, PASSES * P], U8, name="planes%d" % i, align_bytes=64)
             together = 1 if i == 0 else PASSES
             for a in range(PASSES):
-                nc.scalar.activation(
+                interleave = nc.vector.tensor_copy if i == 2 else nc.scalar.copy
+                interleave(
                     out=grouped[:, a, :, :].rearrange("p (c u) j -> p c j u", u=4),
                     in_=raw[(i, a)].rearrange("p j (c u) -> p c j u", u=4),
-                    func=COPY,
                 )
                 weights[(i, a)] = (codes[:, a * P : (a + 1) * P], planes[:, a * P : (a + 1) * P])
                 if (a + 1) % together == 0:
@@ -113,76 +110,69 @@ def tile_moe_block_routed_expert_kernel(tc, xt_words, xt_scales, wa, bw, res, of
                     )
 
         def product(i):
-            for lo, hi in cuts(i):
-                acc[(i, lo)] = psum.tile([P, hi - lo], F32, name="acc%d_%d" % (i, lo))
+            acc[i] = psum.tile([P, J], F32, name="acc%d" % i)
             for a in range(PASSES):
                 codes, plane = weights[(i, a)]
-                for lo, hi in cuts(i):
-                    nc.tensor.matmul_mx(
-                        out=acc[(i, lo)][:],
-                        lhsT=codes.bitcast(FP8X4),
-                        lhsT_scale=plane,
-                        rhs=g_words[a][:, lo:hi].bitcast(FP8X4),
-                        rhs_scale=g_planes[4 * a : P, lo:hi],
-                        start=(a == 0),
-                        stop=(a == PASSES - 1),
-                    )
-
-        def activate(i):
-            gated = held.tile([P, J], F32, name="gated%d" % i, align_bytes=64)
-            act[i] = held.tile([P, J], F32, name="act%d" % i, align_bytes=64)
-            for lo, hi in cuts(i):
-                blocks = (hi - lo) // RUN
-                nc.vector.tensor_tensor(
-                    out=gated[:, lo:hi].rearrange("p (b e) -> p b e", e=RUN),
-                    in0=acc[(i, lo)][:].rearrange("p (b e) -> p b e", e=RUN),
-                    in1=bw_sb[:, i, lo // RUN : hi // RUN].unsqueeze(2).to_broadcast([P, blocks, RUN]),
-                    op=MULT,
+                nc.tensor.matmul_mx(
+                    out=acc[i][:],
+                    lhsT=codes.bitcast(FP8X4),
+                    lhsT_scale=plane,
+                    rhs=g_words[a][:].bitcast(FP8X4),
+                    rhs_scale=g_planes[4 * a : P, :],
+                    start=(a == 0),
+                    stop=(a == PASSES - 1),
                 )
-                nc.scalar.activation(out=act[i][:, lo:hi], in_=gated[:, lo:hi], func=SILU)
+
+        sums = {}
+        spread = {}
+
+        def empty_bank(i):
+            sums[i] = held.tile([P, J], F32, name="sums%d" % i, align_bytes=64)
+            nc.scalar.copy(out=sums[i][:], in_=acc[i][:])
+
+        def spread_bw(i):
+            spread[i] = held.tile([P, J], F32, name="spread%d" % i, align_bytes=64)
+            nc.scalar.copy(
+                out=spread[i][:].rearrange("p (b e) -> p b e", e=RUN),
+                in_=bw_sb[:, i, :].unsqueeze(2).to_broadcast([P, B, RUN]),
+            )
 
         def scatter(i):
-            for lo, hi in cuts(i):
-                nc.vector.tensor_copy(windows[i % 3][:].indirect(offsets[:, lo // 16 : hi // 16]), act[i][:, lo:hi])
+            nc.vector.tensor_tensor(windows[i % 2][:].indirect(offsets[:]), sums[i][:], spread[i][:], MULT)
 
         def finish(i, pieces):
             width = T // pieces
             for h in range(pieces):
                 cols = slice(h * width, (h + 1) * width)
+                act = held.tile([P, width], F32, name="act%d_%d" % (i, h), align_bytes=64)
+                nc.scalar.activation(out=act[:], in_=windows[i % 2][:, cols], func=SILU)
                 total = held.tile([P, width], F32, name="total%d_%d" % (i, h), align_bytes=64)
                 nc.vector.scalar_tensor_tensor(
                     out=total[:],
                     in0=res_sb[i][:, cols],
                     scalar=RES_SCALE,
-                    in1=windows[i % 3][:, cols],
+                    in1=act[:],
                     op0=MULT,
                     op1=ADD,
                 )
                 nc.sync.dma_start(out=out[i * P : (i + 1) * P, cols], in_=total[:])
 
-        def finish_on_gpsimd(i):
-            nc.scalar.activation(out=res_sb[i][:], in_=res_sb[i][:], func=COPY, scale=RES_SCALE)
-            tag = "grouped%d" % (TILES - 1) if i == 0 else "total%d" % i
-            total = held.tile([P, T], F32, name="total%d" % i, tag=tag, align_bytes=64)
-            nc.gpsimd.tensor_tensor(out=total[:], in0=res_sb[i][:], in1=windows[i % 3][:], op=ADD)
-            nc.sync.dma_start(out=out[i * P : (i + 1) * P, :], in_=total[:])
-
-        quantise(0)
-        product(0)
-        activate(0)
-        quantise(1)
-        product(1)
+        for i in (0, 1):
+            quantise(i)
+            product(i)
+            empty_bank(i)
+        for i in range(TILES):
+            spread_bw(i)
         scatter(0)
-        activate(1)
         for i in (2, 3):
             quantise(i)
             product(i)
         scatter(1)
         for i in (2, 3):
-            activate(i)
-        for i in (0, 1):
-            finish_on_gpsimd(i)
+            empty_bank(i)
+        finish(0, 1)
         scatter(2)
+        finish(1, 1)
         scatter(3)
-        finish(2, 1)
+        finish(2, 2)
         finish(3, 2)

from contextlib import ExitStack

import concourse.mybir as mybir

K, T, J, B, N = 1024, 1024, 512, 64, 512
FLOPS = 2 * K * N * J

F32 = mybir.dt.float32
BF16 = mybir.dt.bfloat16
I32 = mybir.dt.int32
U32 = mybir.dt.uint32
U16 = mybir.dt.uint16
U8 = mybir.dt.uint8
FP8X4 = mybir.dt.float8_e4m3fn_x4
MULT = mybir.AluOpType.mult
ADD = mybir.AluOpType.add
SILU = mybir.ActivationFunctionType.Silu

P = 128
PACK = 4
PASSES = K // (P * PACK)
TILES = N // P
RUN = J // B
RES_SCALE = 0.3


def tile_moe_block_routed_expert_kernel(tc, xt_words, xt_scales, wa, bw, res, offs, out):
    nc = tc.nc
    with ExitStack() as ctx:
        held = ctx.enter_context(tc.tile_pool(name="held", bufs=1))
        psum = ctx.enter_context(tc.psum_pool(name="psum", bufs=1))

        offsets = held.tile([P, J // 16], U16, name="offsets")
        x_planes = held.tile([P, T], U8, name="x_planes", align_bytes=64)
        x_words = [held.tile([P, T], U32, name="x_words%d" % a, align_bytes=64) for a in range(PASSES)]
        g_planes = held.tile([P, J], U8, name="g_planes", align_bytes=64)
        g_words = [held.tile([P, J], U32, name="g_words%d" % a, align_bytes=64) for a in range(PASSES)]
        windows = [held.tile([P, T], F32, name="window%d" % i, align_bytes=64) for i in range(2)]
        bw_sb = held.tile([P, TILES, B], F32, name="bw_sb")
        res_sb = [held.tile([P, T], F32, name="res_sb%d" % i, align_bytes=64) for i in range(TILES)]

        warm = held.tile([P, 1], F32, name="warm")
        warm_out = held.tile([P, 1], F32, name="warm_out")
        nc.vector.memset(x_planes[:].bitcast(I32), 0)
        nc.vector.memset(warm[:], 0.0)
        nc.scalar.activation(out=warm_out[:], in_=warm[:], func=SILU)
        for w in windows:
            nc.vector.memset(w[:], 0.0)

        def load_words(a):
            nc.sync.dma_start(
                out=x_words[a][:].bitcast(I32),
                in_=xt_words[a].rearrange("p c r -> p (c r)").bitcast(I32),
            )

        wa_rows = wa.rearrange("(a p j) n -> a p j n", a=PASSES, j=PACK)
        raw = {}

        def load_wa(first, count, a):
            piece = held.tile([P, PACK, count * P], F32, name="raw%d_%d" % (first, a), align_bytes=64)
            nc.sync.dma_start(out=piece[:], in_=wa_rows[a, :, :, first * P : (first + count) * P])
            for i in range(count):
                raw[(first + i, a)] = piece[:, :, i * P : (i + 1) * P]

        def load_res(i):
            nc.sync.dma_start(out=res_sb[i][:], in_=res[i * P : (i + 1) * P, :])

        nc.sync.dma_start(offsets[:], offs)
        load_words(0)
        for q in range(4):
            nc.sync.dma_start(
                out=x_planes[32 * q : 32 * q + 4 * PASSES, :].bitcast(I32),
                in_=xt_scales[:, 4 * q : 4 * q + 4, :].bitcast(I32),
            )
        nc.sync.dma_start(out=bw_sb[:], in_=bw.rearrange("(i p) b -> p i b", p=P))
        load_words(1)
        for a in range(PASSES):
            load_wa(0, 1, a)
        for i in range(1, TILES):
            for a in range(PASSES):
                load_wa(i, 1, a)
        for i in range(TILES):
            load_res(i)

        nc.vector.tensor_copy(g_planes[:], x_planes[:].indirect(offsets[:]))
        for a in range(PASSES):
            nc.vector.tensor_copy(g_words[a][:], x_words[a][:].indirect(offsets[:]))

        weights = {}
        acc = {}

        def quantise(i):
            grouped = held.tile([P, PASSES, P, PACK], BF16, name="grouped%d" % i, align_bytes=64)
            codes = held.tile([P, PASSES * P], U32, name="codes%d" % i, align_bytes=64)
            planes = held.tile([P, PASSES * P], U8, name="planes%d" % i, align_bytes=64)
            together = 1 if i == 0 else PASSES
            for a in range(PASSES):
                interleave = nc.vector.tensor_copy if i == 2 else nc.scalar.copy
                interleave(
                    out=grouped[:, a, :, :].rearrange("p (c u) j -> p c j u", u=4),
                    in_=raw[(i, a)].rearrange("p j (c u) -> p c j u", u=4),
                )
                weights[(i, a)] = (codes[:, a * P : (a + 1) * P], planes[:, a * P : (a + 1) * P])
                if (a + 1) % together == 0:
                    first = a + 1 - together
                    nc.vector.quantize_mx(
                        out=codes[:, first * P : (a + 1) * P].bitcast(FP8X4),
                        scales=planes[:, first * P : (a + 1) * P],
                        in_=grouped[:, first : a + 1, :, :].rearrange("p a c j -> p (a c j)"),
                    )

        def product(i):
            acc[i] = psum.tile([P, J], F32, name="acc%d" % i)
            for a in range(PASSES):
                codes, plane = weights[(i, a)]
                nc.tensor.matmul_mx(
                    out=acc[i][:],
                    lhsT=codes.bitcast(FP8X4),
                    lhsT_scale=plane,
                    rhs=g_words[a][:].bitcast(FP8X4),
                    rhs_scale=g_planes[4 * a : P, :],
                    start=(a == 0),
                    stop=(a == PASSES - 1),
                )

        sums = {}
        spread = {}

        def empty_bank(i):
            sums[i] = held.tile([P, J], F32, name="sums%d" % i, align_bytes=64)
            nc.scalar.copy(out=sums[i][:], in_=acc[i][:])

        def spread_bw(i):
            spread[i] = held.tile([P, J], F32, name="spread%d" % i, align_bytes=64)
            nc.scalar.copy(
                out=spread[i][:].rearrange("p (b e) -> p b e", e=RUN),
                in_=bw_sb[:, i, :].unsqueeze(2).to_broadcast([P, B, RUN]),
            )

        def scatter(i):
            nc.vector.tensor_tensor(windows[i % 2][:].indirect(offsets[:]), sums[i][:], spread[i][:], MULT)

        def finish(i, pieces):
            width = T // pieces
            for h in range(pieces):
                cols = slice(h * width, (h + 1) * width)
                act = held.tile([P, width], F32, name="act%d_%d" % (i, h), align_bytes=64)
                nc.scalar.activation(out=act[:], in_=windows[i % 2][:, cols], func=SILU)
                total = held.tile([P, width], F32, name="total%d_%d" % (i, h), align_bytes=64)
                nc.vector.scalar_tensor_tensor(
                    out=total[:],
                    in0=res_sb[i][:, cols],
                    scalar=RES_SCALE,
                    in1=act[:],
                    op0=MULT,
                    op1=ADD,
                )
                nc.sync.dma_start(out=out[i * P : (i + 1) * P, cols], in_=total[:])

        for i in (0, 1):
            quantise(i)
            product(i)
            empty_bank(i)
        for i in range(TILES):
            spread_bw(i)
        scatter(0)
        for i in (2, 3):
            quantise(i)
            product(i)
        scatter(1)
        for i in (2, 3):
            empty_bank(i)
        finish(0, 1)
        scatter(2)
        finish(1, 1)
        scatter(3)
        finish(2, 2)
        finish(3, 2)
